import numpy as np
import ml_dtypes


def mxq(x, axis, fmt="e4m3"):
    dtype, down = {"e4m3": (ml_dtypes.float8_e4m3fn, 7), "e5m2": (ml_dtypes.float8_e5m2, 14)}[fmt]
    v = np.moveaxis(np.asarray(x, np.float32).astype(ml_dtypes.bfloat16).astype(np.float64), axis, -1)
    blocks = v.reshape(v.shape[:-1] + (-1, 32))
    amax = np.abs(blocks).max(-1, keepdims=True)
    byte = np.maximum(np.where(amax > 0, np.frexp(amax)[1] - 1 + 127, 0) - down, 1)
    scale = np.exp2(byte - 127.0)
    codes = (blocks / scale).astype(np.float32).astype(dtype).astype(np.float64)
    return np.moveaxis((codes * scale).reshape(v.shape), -1, axis)


WIDE = False


def mx_kscale(k):
    if not WIDE:
        return np.ones(k)
    levels = np.array([10, -10, 5, -5, 0])
    if k % 512:
        return np.exp2(np.random.permutation(np.resize(levels, k // 32))).repeat(32)
    a = np.empty((k // 512, 16))
    for p in range(k // 512):
        a[p, :8] = np.random.permutation(np.resize(levels, 8))
        for g in range(8):
            far = levels[np.abs(levels - a[p, g]) >= 10]
            a[p, g + 8] = far[np.random.randint(len(far))]
    return np.exp2(a.ravel()).repeat(32)


def f64(x):
    return np.asarray(x).astype(np.float64)


def striped(idx):
    return np.tile(np.asarray(idx).reshape(-1, 16).T, (8, 1)).astype(np.uint16)


def unstriped(offs):
    return offs[:16].T.reshape(-1).astype(np.int64)


D, T, I, Q, E = 512, 1024, 512, 128, 512


def setup_inputs():
    n = np.random.standard_normal
    idx = np.random.permutation(T)[:I]
    idx2 = np.random.permutation(T)[:I]
    fd = mx_kscale(D)
    fi = mx_kscale(I)
    return {
        "query": (n((D, Q)) * 0.25 / np.sqrt(D) * fd[:, None]).astype(np.float32),
        "keys": (n((D, T)) / fd[:, None]).astype(np.float32),
        "fr": (np.random.uniform(0.1, 0.9, (1, I))).astype(np.float32),
        "fv": (np.random.uniform(0.1, 0.9, (I, 1))).astype(np.float32),
        "size": (np.random.uniform(0.5, 2.0, (1, I)) * fi).astype(np.float32),
        "vals": (n((E, T))).astype(np.float32),
        "vsc": (np.random.uniform(0.5, 2.0, (I, 1)) / fi[:, None]).astype(np.float32),
        "offs": striped(idx),
        "offs2": striped(idx2),
    }


def reference(query, keys, fr, fv, size, vals, vsc, offs, offs2):
    idx = unstriped(offs)
    idx2 = unstriped(offs2)
    km = f64(keys)[:, idx] * (1.0 - f64(fr)) + f64(keys)[:, idx2] * f64(fr)
    queryq = mxq(f64(query), 0, "e4m3")
    kmq = mxq(km, 0, "e4m3")
    a = queryq.T @ kmq
    p = np.exp(a - np.max(a, axis=1, keepdims=True))
    w = p * f64(size) / np.sum(p, axis=1, keepdims=True)
    wt = w.T
    v1 = f64(vals)[:, idx].T
    v2 = f64(vals)[:, idx2].T
    vv = (v1 + (v2 - v1) * f64(fv)) * f64(vsc)
    wtq = mxq(wt, 0, "e4m3")
    vvq = mxq(vv, 0, "e4m3")
    o = wtq.T @ vvq
    return o

@@ -1,0 +1,204 @@
+from contextlib import ExitStack
+
+import concourse.mybir as mybir
+from concourse.masks import make_identity
+
+D, T, I, Q, E = 512, 1024, 512, 128, 512
+FLOPS = 2 * Q * I * D + 2 * Q * I * E
+
+F32 = mybir.dt.float32
+BF16 = mybir.dt.bfloat16
+U32 = mybir.dt.uint32
+U16 = mybir.dt.uint16
+U8 = mybir.dt.uint8
+FP8X4 = mybir.dt.float8_e4m3fn_x4
+ALU = mybir.AluOpType
+ACT = mybir.ActivationFunctionType
+
+P = 128
+PACK = 4
+
+
+def tile_attend_keyframes_kernel(tc, query, keys, fr, fv, size, vals, vsc, offs, offs2, out):
+    nc = tc.nc
+    with ExitStack() as ctx:
+        sb = ctx.enter_context(tc.tile_pool(name="sb", bufs=1))
+        ps = ctx.enter_context(tc.psum_pool(name="ps", bufs=1))
+
+        key_planes = keys.rearrange("(p j) t -> j p t", j=PACK)
+        key = [sb.tile([P, T], F32, name=f"key{j}") for j in range(PACK)]
+        val = [sb.tile([P, T], F32, name=f"val{c}") for c in range(PACK)]
+        list1 = sb.tile([P, I // 16], U16)
+        list2 = sb.tile([P, I // 16], U16)
+        fr_col = sb.tile([P, PACK], F32)
+        fv_col = sb.tile([P, PACK], F32)
+        vsc_col = sb.tile([P, PACK], F32)
+        size_col = sb.tile([P, PACK], F32)
+        q_raw = sb.tile([P, PACK, Q], F32)
+
+        nc.sync.dma_start(out=fr_col[:], in_=fr.rearrange("o (p c) -> p (o c)", c=PACK))
+        nc.sync.dma_start(out=key[0][:], in_=key_planes[0])
+        nc.sync.dma_start(list2[:], offs2)
+        nc.sync.dma_start(list1[:], offs)
+        nc.sync.dma_start(out=key[1][:], in_=key_planes[1])
+        nc.sync.dma_start(out=fv_col[:], in_=fv.rearrange("(p c) o -> p (c o)", c=PACK))
+        nc.sync.dma_start(out=vsc_col[:], in_=vsc.rearrange("(p c) o -> p (c o)", c=PACK))
+        nc.sync.dma_start(out=key[2][:], in_=key_planes[2])
+        nc.sync.dma_start(out=key[3][:], in_=key_planes[3])
+        nc.sync.dma_start(out=size_col[:], in_=size.rearrange("o (p c) -> p (o c)", c=PACK))
+        nc.sync.dma_start(out=val[0][:], in_=vals[0:P, :])
+        nc.sync.dma_start(out=q_raw[:], in_=query.rearrange("(p j) q -> p j q", j=PACK))
+        for c in range(1, PACK):
+            nc.sync.dma_start(out=val[c][:], in_=vals[c * P:(c + 1) * P, :])
+
+        ident = sb.tile([P, P], F32)
+        make_identity(nc, ident[:])
+        ident_bf = sb.tile([P, P], BF16)
+        nc.scalar.activation(ident_bf[:], ident[:], ACT.Copy)
+
+        def spread(col, tag, name):
+            bank = ps.tile([P, PACK, P], F32, tag=tag, name=name)
+            for c in range(PACK):
+                nc.tensor.transpose(bank[:, c, :], col[:, c:c + 1].to_broadcast([P, P]), ident[:])
+            return bank
+
+        def in_slot_order(bank):
+            return bank[:].rearrange("m c p -> m p c")
+
+        def slots4(ap):
+            return ap.rearrange("m (g j r c) -> m g j r c", j=4, r=2, c=4)
+
+        def dealt4(ap):
+            return ap.rearrange("m (j g r c) -> m g j r c", j=4, r=2, c=4)
+
+        def bank4(bank):
+            return bank[:].rearrange("m c (g j r) -> m g j r c", j=4, r=2)
+
+        fr_bank = spread(fr_col, "bank0", "fr_bank")
+        fr_row = sb.tile([P, I], F32)
+        nc.vector.tensor_copy(out=fr_row[:].rearrange("m (p c) -> m p c", c=PACK), in_=in_slot_order(fr_bank))
+        omf_col = sb.tile([P, PACK], F32)
+        nc.scalar.activation(omf_col[:], fr_col[:], ACT.Copy, bias=1.0, scale=-1.0)
+        omf_bank = spread(omf_col, "bank1", "omf_bank")
+
+        k_first = sb.tile([P, PACK, I], F32)
+        k_second = sb.tile([P, PACK, I], F32)
+        k_got = [sb.tile([P, I], F32, name=f"k_got{j}") for j in range(PACK)]
+        omv_col = sb.tile([P, PACK], F32)
+        a_col = sb.tile([P, PACK], F32)
+        b_col = sb.tile([P, PACK], F32)
+        for j in range(PACK):
+            nc.scalar.activation(k_got[j][:], key[j][:].indirect(list1[:]), ACT.Copy)
+            nc.vector.tensor_tensor(k_second[:, j, :], key[j][:].indirect(list2[:]), fr_row[:], ALU.mult)
+            nc.vector.tensor_tensor(
+                k_first[:, j, :].rearrange("m (p c) -> m p c", c=PACK),
+                k_got[j][:].rearrange("m (p c) -> m p c", c=PACK), in_slot_order(omf_bank), ALU.mult)
+            if j == 1:
+                nc.gpsimd.tensor_scalar(omv_col[:], fv_col[:], -1.0, 1.0, ALU.mult, ALU.add)
+                nc.gpsimd.tensor_tensor(b_col[:], fv_col[:], vsc_col[:], ALU.mult)
+                nc.gpsimd.tensor_tensor(a_col[:], omv_col[:], vsc_col[:], ALU.mult)
+        a_bank = spread(a_col, "bank2", "a_bank")
+        b_bank = spread(b_col, "bank3", "b_bank")
+        size_bank = spread(size_col, "bank4", "size_bank")
+
+        q_bf = sb.tile([P, Q, PACK], BF16, align_bytes=64)
+        nc.vector.tensor_copy(
+            out=q_bf[:].rearrange("p (c i) j -> p c j i", i=4), in_=q_raw[:].rearrange("p j (c i) -> p c j i", i=4))
+        km_bf = sb.tile([P, I, PACK], BF16, align_bytes=64)
+        nc.vector.tensor_tensor(
+            km_bf[:].rearrange("p (c i) j -> p c j i", i=4),
+            k_first[:].rearrange("p j (c i) -> p c j i", i=4),
+            k_second[:].rearrange("p j (c i) -> p c j i", i=4), ALU.add)
+        q_codes = sb.tile([P, Q], U32, align_bytes=64)
+        q_scales = sb.tile([P, Q], U8, align_bytes=64)
+        nc.vector.quantize_mx(out=q_codes[:].bitcast(FP8X4), scales=q_scales[:],
+                              in_=q_bf[:].rearrange("p q j -> p (q j)"))
+        km_codes = sb.tile([P, I], U32, align_bytes=64)
+        km_scales = sb.tile([P, I], U8, align_bytes=64)
+        nc.vector.quantize_mx(out=km_codes[:].bitcast(FP8X4), scales=km_scales[:],
+                              in_=km_bf[:].rearrange("p i j -> p (i j)"))
+        scores = ps.tile([P, I], F32, tag="bank0", name="scores")
+        nc.tensor.matmul_mx(out=scores[:], lhsT=q_codes[:].bitcast(FP8X4), lhsT_scale=q_scales[:],
+                            rhs=km_codes[:].bitcast(FP8X4), rhs_scale=km_scales[:], start=True, stop=True)
+
+        vv_codes = sb.tile([P, E], U32, align_bytes=64)
+        vv_scales = sb.tile([P, E], U8, align_bytes=64)
+
+        def gather_values(c):
+            got1 = sb.tile([P, I], F32, name=f"v_got1_{c}")
+            got2 = sb.tile([P, I], F32, name=f"v_got2_{c}")
+            nc.scalar.activation(got1[:], val[c][:].indirect(list1[:]), ACT.Copy)
+            nc.scalar.activation(got2[:], val[c][:].indirect(list2[:]), ACT.Copy)
+            return got1, got2
+
+        def weigh_and_turn(c, got):
+            part1 = sb.tile([P, I], F32, name=f"v_part1_{c}")
+            part2 = sb.tile([P, I], F32, name=f"v_part2_{c}")
+            nc.vector.tensor_tensor(dealt4(part1[:]), slots4(got[0][:]), bank4(a_bank), ALU.mult)
+            nc.vector.tensor_tensor(dealt4(part2[:]), slots4(got[1][:]), bank4(b_bank), ALU.mult)
+            turned = ps.tile([P, PACK, P], F32, tag=f"turn{c % 2}", name=f"turned{c}")
+            for j in range(PACK):
+                nc.tensor.matmul(turned[:, j, :], lhsT=part1[:, j * P:(j + 1) * P], rhs=ident[:],
+                                 start=True, stop=False, is_transpose=True)
+                nc.tensor.matmul(turned[:, j, :], lhsT=part2[:, j * P:(j + 1) * P], rhs=ident[:],
+                                 start=False, stop=True, is_transpose=True)
+            return turned
+
+        def quantise_values(c, turned, copy):
+            vv_bf = sb.tile([P, P, PACK], BF16, name=f"vv_bf{c}", align_bytes=64)
+            copy(out=vv_bf[:], in_=turned[:].rearrange("p j e -> p e j"))
+            nc.vector.quantize_mx(out=vv_codes[:, c * P:(c + 1) * P].bitcast(FP8X4),
+                                  scales=vv_scales[:, c * P:(c + 1) * P],
+                                  in_=vv_bf[:].rearrange("p e j -> p (e j)"))
+
+        got0 = gather_values(0)
+        got1 = gather_values(1)
+        turned0 = weigh_and_turn(0, got0)
+
+        neg_max = sb.tile([P, 1], F32)
+        nc.vector.tensor_reduce(neg_max[:], scores[:], mybir.AxisListType.X, ALU.max, negate=True)
+        got2 = gather_values(2)
+        p_exp = sb.tile([P, I], F32)
+        row_sum = sb.tile([P, 1], F32)
+        nc.scalar.activation(p_exp[:], scores[:], ACT.Exp, bias=neg_max[:], scale=1.0, accum_out=row_sum[:])
+        turned1 = weigh_and_turn(1, got1)
+        got3 = gather_values(3)
+        inv_sum = sb.tile([P, 1], F32)
+        nc.vector.reciprocal(inv_sum[:], row_sum[:])
+        p_size = sb.tile([P, I], F32)
+        nc.vector.tensor_tensor(dealt4(p_size[:]), slots4(p_exp[:]), bank4(size_bank), ALU.mult)
+        w = sb.tile([P, I], BF16)
+        nc.vector.tensor_scalar(w[:], p_size[:], inv_sum[:], None, ALU.mult)
+        w_turned = ps.tile([P, PACK, Q], BF16, tag="bank1", name="w_turned")
+        for j in range(PACK):
+            nc.tensor.transpose(w_turned[:, j, :], w[:, j * P:(j + 1) * P], ident_bf[:])
+        quantise_values(0, turned0, nc.scalar.copy)
+        turned2 = weigh_and_turn(2, got2)
+        quantise_values(1, turned1, nc.scalar.copy)
+        turned3 = weigh_and_turn(3, got3)
+        wt_bf = sb.tile([P, Q, PACK], BF16, align_bytes=64)
+        nc.vector.tensor_copy(out=wt_bf[:], in_=w_turned[:].rearrange("p j q -> p q j"))
+        wt_codes = sb.tile([P, Q], U32, align_bytes=64)
+        wt_scales = sb.tile([P, Q], U8, align_bytes=64)
+        nc.vector.quantize_mx(out=wt_codes[:].bitcast(FP8X4), scales=wt_scales[:],
+                              in_=wt_bf[:].rearrange("p q j -> p (q j)"))
+        quantise_values(2, turned2, nc.scalar.copy)
+        quantise_values(3, turned3, nc.scalar.copy)
+
+        def product(acc, e0, n):
+            nc.tensor.matmul_mx(out=acc, lhsT=wt_codes[:].bitcast(FP8X4), lhsT_scale=wt_scales[:],
+                                rhs=vv_codes[:, e0:e0 + n].bitcast(FP8X4), rhs_scale=vv_scales[:, e0:e0 + n],
+                                start=True, stop=True)
+
+        half = E // 2
+        acc0 = ps.tile([P, half], F32, tag="bank7", name="acc0")
+        acc1 = ps.tile([P, half], F32, tag="bank4", name="acc1")
+        product(acc0[:], 0, half)
+        res0 = sb.tile([P, half], F32)
+        nc.vector.tensor_copy(out=res0[:], in_=acc0[:])
+        nc.sync.dma_start(out=out[:, 0:half], in_=res0[:])
+        product(acc1[:, 0:P], half, P)
+        product(acc1[:, P:half], half + P, P)
+        res1 = sb.tile([P, half], F32)
+        nc.vector.tensor_copy(out=res1[:], in_=acc1[:])
+        nc.sync.dma_start(out=out[:, half:E], in_=res1[:])

@@ -17,6 +17,7 @@ ACT = mybir.ActivationFunctionType
 
 P = 128
 PACK = 4
+TURN_BANKS = ("bank5", "bank6", "bank7", "bank0")
 
 
 def tile_attend_keyframes_kernel(tc, query, keys, fr, fv, size, vals, vsc, offs, offs2, out):
@@ -26,8 +27,8 @@ def tile_attend_keyframes_kernel(tc, query, keys, fr, fv, size, vals, vsc, offs,
         ps = ctx.enter_context(tc.psum_pool(name="ps", bufs=1))
 
         key_planes = keys.rearrange("(p j) t -> j p t", j=PACK)
-        key = [sb.tile([P, T], F32, name=f"key{j}") for j in range(PACK)]
-        val = [sb.tile([P, T], F32, name=f"val{c}") for c in range(PACK)]
+        key = [sb.tile([P, T], F32, tag=f"key{j}", name=f"key{j}") for j in range(PACK)]
+        val = [sb.tile([P, T], F32, tag=f"val{c}", name=f"val{c}", align_bytes=64) for c in range(PACK)]
         list1 = sb.tile([P, I // 16], U16)
         list2 = sb.tile([P, I // 16], U16)
         fr_col = sb.tile([P, PACK], F32)
@@ -81,8 +82,8 @@ def tile_attend_keyframes_kernel(tc, query, keys, fr, fv, size, vals, vsc, offs,
         nc.scalar.activation(omf_col[:], fr_col[:], ACT.Copy, bias=1.0, scale=-1.0)
         omf_bank = spread(omf_col, "bank1", "omf_bank")
 
-        k_first = sb.tile([P, PACK, I], F32)
-        k_second = sb.tile([P, PACK, I], F32)
+        k_first = sb.tile([P, PACK, I], F32, tag="key0")
+        k_second = sb.tile([P, PACK, I], F32, tag="k_second")
         k_got = [sb.tile([P, I], F32, name=f"k_got{j}") for j in range(PACK)]
         omv_col = sb.tile([P, PACK], F32)
         a_col = sb.tile([P, PACK], F32)
@@ -104,7 +105,7 @@ def tile_attend_keyframes_kernel(tc, query, keys, fr, fv, size, vals, vsc, offs,
         q_bf = sb.tile([P, Q, PACK], BF16, align_bytes=64)
         nc.vector.tensor_copy(
             out=q_bf[:].rearrange("p (c i) j -> p c j i", i=4), in_=q_raw[:].rearrange("p j (c i) -> p c j i", i=4))
-        km_bf = sb.tile([P, I, PACK], BF16, align_bytes=64)
+        km_bf = sb.tile([P, I, PACK], BF16, tag="km_bf", align_bytes=64)
         nc.vector.tensor_tensor(
             km_bf[:].rearrange("p (c i) j -> p c j i", i=4),
             k_first[:].rearrange("p j (c i) -> p c j i", i=4),
@@ -124,45 +125,45 @@ def tile_attend_keyframes_kernel(tc, query, keys, fr, fv, size, vals, vsc, offs,
         vv_codes = sb.tile([P, E], U32, align_bytes=64)
         vv_scales = sb.tile([P, E], U8, align_bytes=64)
 
-        def gather_values(c):
-            got1 = sb.tile([P, I], F32, name=f"v_got1_{c}")
-            got2 = sb.tile([P, I], F32, name=f"v_got2_{c}")
-            nc.scalar.activation(got1[:], val[c][:].indirect(list1[:]), ACT.Copy)
-            nc.scalar.activation(got2[:], val[c][:].indirect(list2[:]), ACT.Copy)
-            return got1, got2
+        def gather_values(c, tag):
+            got = sb.tile([P, 2, I], F32, tag=tag, name=f"v_got{c}")
+            nc.scalar.activation(got[:, 0, :], val[c][:].indirect(list1[:]), ACT.Copy)
+            nc.scalar.activation(got[:, 1, :], val[c][:].indirect(list2[:]), ACT.Copy)
+            return got
 
-        def weigh_and_turn(c, got):
-            part1 = sb.tile([P, I], F32, name=f"v_part1_{c}")
-            part2 = sb.tile([P, I], F32, name=f"v_part2_{c}")
-            nc.vector.tensor_tensor(dealt4(part1[:]), slots4(got[0][:]), bank4(a_bank), ALU.mult)
-            nc.vector.tensor_tensor(dealt4(part2[:]), slots4(got[1][:]), bank4(b_bank), ALU.mult)
-            turned = ps.tile([P, PACK, P], F32, tag=f"turn{c % 2}", name=f"turned{c}")
+        def weigh_and_turn(c, got, tag1, tag2):
+            part1 = sb.tile([P, I], F32, tag=tag1, name=f"v_part1_{c}", align_bytes=64)
+            part2 = sb.tile([P, I], F32, tag=tag2, name=f"v_part2_{c}")
+            nc.vector.tensor_tensor(dealt4(part1[:]), slots4(got[:, 0, :]), bank4(a_bank), ALU.mult)
+            nc.vector.tensor_tensor(dealt4(part2[:]), slots4(got[:, 1, :]), bank4(b_bank), ALU.mult)
+            turned = ps.tile([P, PACK, P], F32, tag=TURN_BANKS[c], name=f"turned{c}")
             for j in range(PACK):
                 nc.tensor.matmul(turned[:, j, :], lhsT=part1[:, j * P:(j + 1) * P], rhs=ident[:],
-                                 start=True, stop=False, is_transpose=True)
+                                 start=(j == 0), stop=False, is_transpose=True)
+            for j in range(PACK):
                 nc.tensor.matmul(turned[:, j, :], lhsT=part2[:, j * P:(j + 1) * P], rhs=ident[:],
-                                 start=False, stop=True, is_transpose=True)
+                                 start=False, stop=(j == PACK - 1), is_transpose=True)
             return turned
 
         def quantise_values(c, turned, copy):
-            vv_bf = sb.tile([P, P, PACK], BF16, name=f"vv_bf{c}", align_bytes=64)
-            copy(out=vv_bf[:], in_=turned[:].rearrange("p j e -> p e j"))
+            vv_bf = rounded[:, c, :].rearrange("p (e j) -> p e j", j=PACK)
+            copy(out=vv_bf, in_=turned[:].rearrange("p j e -> p e j"))
             nc.vector.quantize_mx(out=vv_codes[:, c * P:(c + 1) * P].bitcast(FP8X4),
                                   scales=vv_scales[:, c * P:(c + 1) * P],
-                                  in_=vv_bf[:].rearrange("p e j -> p (e j)"))
+                                  in_=rounded[:, c, :])
 
-        got0 = gather_values(0)
-        got1 = gather_values(1)
-        turned0 = weigh_and_turn(0, got0)
+        got0 = gather_values(0, "got0")
+        got1 = gather_values(1, "got1")
+        turned0 = weigh_and_turn(0, got0, "km_bf", "key0")
 
-        neg_max = sb.tile([P, 1], F32)
+        neg_max = sb.tile([P, 1], F32, tag="neg_max")
         nc.vector.tensor_reduce(neg_max[:], scores[:], mybir.AxisListType.X, ALU.max, negate=True)
-        got2 = gather_values(2)
+        got2 = gather_values(2, "got2")
         p_exp = sb.tile([P, I], F32)
         row_sum = sb.tile([P, 1], F32)
         nc.scalar.activation(p_exp[:], scores[:], ACT.Exp, bias=neg_max[:], scale=1.0, accum_out=row_sum[:])
-        turned1 = weigh_and_turn(1, got1)
-        got3 = gather_values(3)
+        turned1 = weigh_and_turn(1, got1, "part1_1", "k_second")
+        got3 = gather_values(3, "neg_max")
         inv_sum = sb.tile([P, 1], F32)
         nc.vector.reciprocal(inv_sum[:], row_sum[:])
         p_size = sb.tile([P, I], F32)
@@ -172,17 +173,18 @@ def tile_attend_keyframes_kernel(tc, query, keys, fr, fv, size, vals, vsc, offs,
         w_turned = ps.tile([P, PACK, Q], BF16, tag="bank1", name="w_turned")
         for j in range(PACK):
             nc.tensor.transpose(w_turned[:, j, :], w[:, j * P:(j + 1) * P], ident_bf[:])
+        turned2 = weigh_and_turn(2, got2, "part1_2", "part2_2")
+        turned3 = weigh_and_turn(3, got3, "part1_3", "part2_3")
+        rounded = sb.tile([P, PACK + 1, PACK * P], BF16, tag="val3", align_bytes=64)
         quantise_values(0, turned0, nc.scalar.copy)
-        turned2 = weigh_and_turn(2, got2)
-        quantise_values(1, turned1, nc.scalar.copy)
-        turned3 = weigh_and_turn(3, got3)
-        wt_bf = sb.tile([P, Q, PACK], BF16, align_bytes=64)
-        nc.vector.tensor_copy(out=wt_bf[:], in_=w_turned[:].rearrange("p j q -> p q j"))
+        wt_bf = rounded[:, PACK, :]
+        nc.scalar.copy(out=wt_bf.rearrange("p (q j) -> p q j", j=PACK), in_=w_turned[:].rearrange("p j q -> p q j"))
         wt_codes = sb.tile([P, Q], U32, align_bytes=64)
         wt_scales = sb.tile([P, Q], U8, align_bytes=64)
         nc.vector.quantize_mx(out=wt_codes[:].bitcast(FP8X4), scales=wt_scales[:],
-                              in_=wt_bf[:].rearrange("p q j -> p (q j)"))
-        quantise_values(2, turned2, nc.scalar.copy)
+                              in_=wt_bf)
+        quantise_values(1, turned1, nc.scalar.copy)
+        quantise_values(2, turned2, nc.vector.tensor_copy)
         quantise_values(3, turned3, nc.scalar.copy)
 
         def product(acc, e0, n):
@@ -190,15 +192,9 @@ def tile_attend_keyframes_kernel(tc, query, keys, fr, fv, size, vals, vsc, offs,
                                 rhs=vv_codes[:, e0:e0 + n].bitcast(FP8X4), rhs_scale=vv_scales[:, e0:e0 + n],
                                 start=True, stop=True)
 
-        half = E // 2
-        acc0 = ps.tile([P, half], F32, tag="bank7", name="acc0")
-        acc1 = ps.tile([P, half], F32, tag="bank4", name="acc1")
-        product(acc0[:], 0, half)
-        res0 = sb.tile([P, half], F32)
-        nc.vector.tensor_copy(out=res0[:], in_=acc0[:])
-        nc.sync.dma_start(out=out[:, 0:half], in_=res0[:])
-        product(acc1[:, 0:P], half, P)
-        product(acc1[:, P:half], half + P, P)
-        res1 = sb.tile([P, half], F32)
-        nc.vector.tensor_copy(out=res1[:], in_=acc1[:])
-        nc.sync.dma_start(out=out[:, half:E], in_=res1[:])
+        for e0, n, tag in ((0, 2 * P, "bank4"), (2 * P, P, "bank5"), (3 * P, P, "bank6")):
+            acc = ps.tile([P, n], F32, tag=tag, name=f"acc{e0}")
+            product(acc[:], e0, n)
+            res = sb.tile([P, n], F32, name=f"res{e0}")
+            nc.vector.tensor_copy(out=res[:], in_=acc[:])
+            nc.sync.dma_start(out=out[:, e0:e0 + n], in_=res[:])

@@ -145,9 +145,11 @@ def tile_attend_keyframes_kernel(tc, query, keys, fr, fv, size, vals, vsc, offs,
                                  start=False, stop=(j == PACK - 1), is_transpose=True)
             return turned
 
-        def quantise_values(c, turned, copy):
+        def round_values(c, turned, copy):
             vv_bf = rounded[:, c, :].rearrange("p (e j) -> p e j", j=PACK)
             copy(out=vv_bf, in_=turned[:].rearrange("p j e -> p e j"))
+
+        def quantise_values(c):
             nc.vector.quantize_mx(out=vv_codes[:, c * P:(c + 1) * P].bitcast(FP8X4),
                                   scales=vv_scales[:, c * P:(c + 1) * P],
                                   in_=rounded[:, c, :])
@@ -176,25 +178,35 @@ def tile_attend_keyframes_kernel(tc, query, keys, fr, fv, size, vals, vsc, offs,
         turned2 = weigh_and_turn(2, got2, "part1_2", "part2_2")
         turned3 = weigh_and_turn(3, got3, "part1_3", "part2_3")
         rounded = sb.tile([P, PACK + 1, PACK * P], BF16, tag="val3", align_bytes=64)
-        quantise_values(0, turned0, nc.scalar.copy)
+        round_values(2, turned2, nc.vector.tensor_copy)
+        round_values(0, turned0, nc.scalar.copy)
+        quantise_values(0)
         wt_bf = rounded[:, PACK, :]
         nc.scalar.copy(out=wt_bf.rearrange("p (q j) -> p q j", j=PACK), in_=w_turned[:].rearrange("p j q -> p q j"))
         wt_codes = sb.tile([P, Q], U32, align_bytes=64)
         wt_scales = sb.tile([P, Q], U8, align_bytes=64)
         nc.vector.quantize_mx(out=wt_codes[:].bitcast(FP8X4), scales=wt_scales[:],
                               in_=wt_bf)
-        quantise_values(1, turned1, nc.scalar.copy)
-        quantise_values(2, turned2, nc.vector.tensor_copy)
-        quantise_values(3, turned3, nc.scalar.copy)
+        round_values(1, turned1, nc.scalar.copy)
+        quantise_values(1)
+        round_values(3, turned3, nc.scalar.copy)
+        quantise_values(2)
+        quantise_values(3)
 
         def product(acc, e0, n):
             nc.tensor.matmul_mx(out=acc, lhsT=wt_codes[:].bitcast(FP8X4), lhsT_scale=wt_scales[:],
                                 rhs=vv_codes[:, e0:e0 + n].bitcast(FP8X4), rhs_scale=vv_scales[:, e0:e0 + n],
                                 start=True, stop=True)
 
-        for e0, n, tag in ((0, 2 * P, "bank4"), (2 * P, P, "bank5"), (3 * P, P, "bank6")):
-            acc = ps.tile([P, n], F32, tag=tag, name=f"acc{e0}")
-            product(acc[:], e0, n)
-            res = sb.tile([P, n], F32, name=f"res{e0}")
-            nc.vector.tensor_copy(out=res[:], in_=acc[:])
-            nc.sync.dma_start(out=out[:, e0:e0 + n], in_=res[:])
+        half = E // 2
+        acc0 = ps.tile([P, half], F32, tag="bank4", name="acc0")
+        product(acc0[:], 0, half)
+        res0 = sb.tile([P, half], F32)
+        nc.scalar.copy(out=res0[:], in_=acc0[:])
+        nc.scalar.dma_start(out=out[:, 0:half], in_=res0[:])
+        acc1 = ps.tile([P, half], F32, tag="bank5", name="acc1")
+        product(acc1[:, 0:P], half, P)
+        product(acc1[:, P:half], half + P, P)
+        res1 = sb.tile([P, half], F32)
+        nc.vector.tensor_copy(out=res1[:], in_=acc1[:])
+        nc.sync.dma_start(out=out[:, half:E], in_=res1[:])

@@ -34,7 +34,7 @@ def tile_attend_keyframes_kernel(tc, query, keys, fr, fv, size, vals, vsc, offs,
         fr_col = sb.tile([P, PACK], F32)
         fv_col = sb.tile([P, PACK], F32)
         vsc_col = sb.tile([P, PACK], F32)
-        size_col = sb.tile([P, PACK], F32)
+        size_row = sb.tile([P, I], F32)
         q_raw = sb.tile([P, PACK, Q], F32)
 
         nc.sync.dma_start(out=fr_col[:], in_=fr.rearrange("o (p c) -> p (o c)", c=PACK))
@@ -46,11 +46,11 @@ def tile_attend_keyframes_kernel(tc, query, keys, fr, fv, size, vals, vsc, offs,
         nc.sync.dma_start(out=vsc_col[:], in_=vsc.rearrange("(p c) o -> p (c o)", c=PACK))
         nc.sync.dma_start(out=key[2][:], in_=key_planes[2])
         nc.sync.dma_start(out=key[3][:], in_=key_planes[3])
-        nc.sync.dma_start(out=size_col[:], in_=size.rearrange("o (p c) -> p (o c)", c=PACK))
         nc.sync.dma_start(out=val[0][:], in_=vals[0:P, :])
         nc.sync.dma_start(out=q_raw[:], in_=query.rearrange("(p j) q -> p j q", j=PACK))
         for c in range(1, PACK):
             nc.sync.dma_start(out=val[c][:], in_=vals[c * P:(c + 1) * P, :])
+        nc.sync.dma_start(out=size_row[:], in_=size.to_broadcast([P, I]))
 
         ident = sb.tile([P, P], F32)
         make_identity(nc, ident[:])
@@ -100,7 +100,6 @@ def tile_attend_keyframes_kernel(tc, query, keys, fr, fv, size, vals, vsc, offs,
                 nc.gpsimd.tensor_tensor(a_col[:], omv_col[:], vsc_col[:], ALU.mult)
         a_bank = spread(a_col, "bank2", "a_bank")
         b_bank = spread(b_col, "bank3", "b_bank")
-        size_bank = spread(size_col, "bank4", "size_bank")
 
         q_bf = sb.tile([P, Q, PACK], BF16, align_bytes=64)
         nc.vector.tensor_copy(
@@ -125,6 +124,9 @@ def tile_attend_keyframes_kernel(tc, query, keys, fr, fv, size, vals, vsc, offs,
         vv_codes = sb.tile([P, E], U32, align_bytes=64)
         vv_scales = sb.tile([P, E], U8, align_bytes=64)
 
+        by_vector = sb.tile([P, PACK * P], BF16, align_bytes=64)
+        vv_bf = {2: by_vector[:]}
+
         def gather_values(c, tag):
             got = sb.tile([P, 2, I], F32, tag=tag, name=f"v_got{c}")
             nc.scalar.activation(got[:, 0, :], val[c][:].indirect(list1[:]), ACT.Copy)
@@ -135,7 +137,11 @@ def tile_attend_keyframes_kernel(tc, query, keys, fr, fv, size, vals, vsc, offs,
             part1 = sb.tile([P, I], F32, tag=tag1, name=f"v_part1_{c}", align_bytes=64)
             part2 = sb.tile([P, I], F32, tag=tag2, name=f"v_part2_{c}")
             nc.vector.tensor_tensor(dealt4(part1[:]), slots4(got[:, 0, :]), bank4(a_bank), ALU.mult)
-            nc.vector.tensor_tensor(dealt4(part2[:]), slots4(got[:, 1, :]), bank4(b_bank), ALU.mult)
+            step = PACK // 2 if c == PACK - 1 else PACK
+            for j0 in range(0, PACK, step):
+                places = slice(j0, j0 + step)
+                nc.vector.tensor_tensor(dealt4(part2[:])[:, :, places], slots4(got[:, 1, :])[:, :, places],
+                                        bank4(b_bank)[:, :, places], ALU.mult)
             turned = ps.tile([P, PACK, P], F32, tag=TURN_BANKS[c], name=f"turned{c}")
             for j in range(PACK):
                 nc.tensor.matmul(turned[:, j, :], lhsT=part1[:, j * P:(j + 1) * P], rhs=ident[:],
@@ -146,13 +152,12 @@ def tile_attend_keyframes_kernel(tc, query, keys, fr, fv, size, vals, vsc, offs,
             return turned
 
         def round_values(c, turned, copy):
-            vv_bf = rounded[:, c, :].rearrange("p (e j) -> p e j", j=PACK)
-            copy(out=vv_bf, in_=turned[:].rearrange("p j e -> p e j"))
+            copy(out=vv_bf[c].rearrange("p (e j) -> p e j", j=PACK), in_=turned[:].rearrange("p j e -> p e j"))
 
         def quantise_values(c):
             nc.vector.quantize_mx(out=vv_codes[:, c * P:(c + 1) * P].bitcast(FP8X4),
                                   scales=vv_scales[:, c * P:(c + 1) * P],
-                                  in_=rounded[:, c, :])
+                                  in_=vv_bf[c])
 
         got0 = gather_values(0, "got0")
         got1 = gather_values(1, "got1")
@@ -166,22 +171,26 @@ def tile_attend_keyframes_kernel(tc, query, keys, fr, fv, size, vals, vsc, offs,
         nc.scalar.activation(p_exp[:], scores[:], ACT.Exp, bias=neg_max[:], scale=1.0, accum_out=row_sum[:])
         turned1 = weigh_and_turn(1, got1, "part1_1", "k_second")
         got3 = gather_values(3, "neg_max")
-        inv_sum = sb.tile([P, 1], F32)
+        inv_sum = sb.tile([P, 1], F32, tag="got1")
         nc.vector.reciprocal(inv_sum[:], row_sum[:])
         p_size = sb.tile([P, I], F32)
-        nc.vector.tensor_tensor(dealt4(p_size[:]), slots4(p_exp[:]), bank4(size_bank), ALU.mult)
+        nc.gpsimd.tensor_tensor(p_size[:], p_exp[:], size_row[:], ALU.mult)
         w = sb.tile([P, I], BF16)
-        nc.vector.tensor_scalar(w[:], p_size[:], inv_sum[:], None, ALU.mult)
+        nc.gpsimd.tensor_scalar(dealt4(w[:]), slots4(p_size[:]), inv_sum[:], 0.0, ALU.mult, ALU.add)
         w_turned = ps.tile([P, PACK, Q], BF16, tag="bank1", name="w_turned")
         for j in range(PACK):
             nc.tensor.transpose(w_turned[:, j, :], w[:, j * P:(j + 1) * P], ident_bf[:])
         turned2 = weigh_and_turn(2, got2, "part1_2", "part2_2")
         turned3 = weigh_and_turn(3, got3, "part1_3", "part2_3")
-        rounded = sb.tile([P, PACK + 1, PACK * P], BF16, tag="val3", align_bytes=64)
+        by_scalar = sb.tile([P, 4, PACK * P], BF16, tag="val3", align_bytes=64)
+        vv_bf[0] = by_scalar[:, 3, :]
+        vv_bf[1] = by_scalar[:, 1, :]
+        vv_bf[3] = by_scalar[:, 2, :]
         round_values(2, turned2, nc.vector.tensor_copy)
         round_values(0, turned0, nc.scalar.copy)
+        quantise_values(2)
         quantise_values(0)
-        wt_bf = rounded[:, PACK, :]
+        wt_bf = by_scalar[:, 0, :]
         nc.scalar.copy(out=wt_bf.rearrange("p (q j) -> p q j", j=PACK), in_=w_turned[:].rearrange("p j q -> p q j"))
         wt_codes = sb.tile([P, Q], U32, align_bytes=64)
         wt_scales = sb.tile([P, Q], U8, align_bytes=64)
@@ -190,7 +199,6 @@ def tile_attend_keyframes_kernel(tc, query, keys, fr, fv, size, vals, vsc, offs,
         round_values(1, turned1, nc.scalar.copy)
         quantise_values(1)
         round_values(3, turned3, nc.scalar.copy)
-        quantise_values(2)
         quantise_values(3)
 
         def product(acc, e0, n):
@@ -198,15 +206,15 @@ def tile_attend_keyframes_kernel(tc, query, keys, fr, fv, size, vals, vsc, offs,
                                 rhs=vv_codes[:, e0:e0 + n].bitcast(FP8X4), rhs_scale=vv_scales[:, e0:e0 + n],
                                 start=True, stop=True)
 
-        half = E // 2
-        acc0 = ps.tile([P, half], F32, tag="bank4", name="acc0")
-        product(acc0[:], 0, half)
-        res0 = sb.tile([P, half], F32)
+        last = E - P
+        acc0 = ps.tile([P, last], F32, tag="bank4", name="acc0")
+        product(acc0[:, 0:2 * P], 0, 2 * P)
+        product(acc0[:, 2 * P:last], 2 * P, P)
+        res0 = sb.tile([P, last], F32)
         nc.scalar.copy(out=res0[:], in_=acc0[:])
-        nc.scalar.dma_start(out=out[:, 0:half], in_=res0[:])
-        acc1 = ps.tile([P, half], F32, tag="bank5", name="acc1")
-        product(acc1[:, 0:P], half, P)
-        product(acc1[:, P:half], half + P, P)
-        res1 = sb.tile([P, half], F32)
+        nc.scalar.dma_start(out=out[:, 0:last], in_=res0[:])
+        acc1 = ps.tile([P, P], F32, tag="bank5", name="acc1")
+        product(acc1[:], last, P)
+        res1 = sb.tile([P, P], F32)
         nc.vector.tensor_copy(out=res1[:], in_=acc1[:])
-        nc.sync.dma_start(out=out[:, half:E], in_=res1[:])
+        nc.sync.dma_start(out=out[:, last:E], in_=res1[:])

@@ -34,7 +34,7 @@ def tile_attend_keyframes_kernel(tc, query, keys, fr, fv, size, vals, vsc, offs,
         fr_col = sb.tile([P, PACK], F32)
         fv_col = sb.tile([P, PACK], F32)
         vsc_col = sb.tile([P, PACK], F32)
-        size_row = sb.tile([P, I], F32)
+        size_col = sb.tile([P, PACK], F32)
         q_raw = sb.tile([P, PACK, Q], F32)
 
         nc.sync.dma_start(out=fr_col[:], in_=fr.rearrange("o (p c) -> p (o c)", c=PACK))
@@ -46,11 +46,11 @@ def tile_attend_keyframes_kernel(tc, query, keys, fr, fv, size, vals, vsc, offs,
         nc.sync.dma_start(out=vsc_col[:], in_=vsc.rearrange("(p c) o -> p (c o)", c=PACK))
         nc.sync.dma_start(out=key[2][:], in_=key_planes[2])
         nc.sync.dma_start(out=key[3][:], in_=key_planes[3])
+        nc.sync.dma_start(out=size_col[:], in_=size.rearrange("o (p c) -> p (o c)", c=PACK))
         nc.sync.dma_start(out=val[0][:], in_=vals[0:P, :])
         nc.sync.dma_start(out=q_raw[:], in_=query.rearrange("(p j) q -> p j q", j=PACK))
         for c in range(1, PACK):
             nc.sync.dma_start(out=val[c][:], in_=vals[c * P:(c + 1) * P, :])
-        nc.sync.dma_start(out=size_row[:], in_=size.to_broadcast([P, I]))
 
         ident = sb.tile([P, P], F32)
         make_identity(nc, ident[:])
@@ -100,6 +100,10 @@ def tile_attend_keyframes_kernel(tc, query, keys, fr, fv, size, vals, vsc, offs,
                 nc.gpsimd.tensor_tensor(a_col[:], omv_col[:], vsc_col[:], ALU.mult)
         a_bank = spread(a_col, "bank2", "a_bank")
         b_bank = spread(b_col, "bank3", "b_bank")
+        size_bank = ps.tile([P, I], F32, tag="bank4", name="size_bank")
+        size_places = size_bank[:].rearrange("m (j g r c) -> m c g j r", j=4, r=2, c=4)
+        for c in range(PACK):
+            nc.tensor.transpose(size_places[:, c], size_col[:, c:c + 1].to_broadcast([P, P]), ident[:])
 
         q_bf = sb.tile([P, Q, PACK], BF16, align_bytes=64)
         nc.vector.tensor_copy(
@@ -123,9 +127,6 @@ def tile_attend_keyframes_kernel(tc, query, keys, fr, fv, size, vals, vsc, offs,
 
         vv_codes = sb.tile([P, E], U32, align_bytes=64)
         vv_scales = sb.tile([P, E], U8, align_bytes=64)
-
-        by_vector = sb.tile([P, PACK * P], BF16, align_bytes=64)
-        vv_bf = {2: by_vector[:]}
 
         def gather_values(c, tag):
             got = sb.tile([P, 2, I], F32, tag=tag, name=f"v_got{c}")
@@ -152,12 +153,13 @@ def tile_attend_keyframes_kernel(tc, query, keys, fr, fv, size, vals, vsc, offs,
             return turned
 
         def round_values(c, turned, copy):
-            copy(out=vv_bf[c].rearrange("p (e j) -> p e j", j=PACK), in_=turned[:].rearrange("p j e -> p e j"))
+            vv_bf = rounded[:, c, :].rearrange("p (e j) -> p e j", j=PACK)
+            copy(out=vv_bf, in_=turned[:].rearrange("p j e -> p e j"))
 
         def quantise_values(c):
             nc.vector.quantize_mx(out=vv_codes[:, c * P:(c + 1) * P].bitcast(FP8X4),
                                   scales=vv_scales[:, c * P:(c + 1) * P],
-                                  in_=vv_bf[c])
+                                  in_=rounded[:, c, :])
 
         got0 = gather_values(0, "got0")
         got1 = gather_values(1, "got1")
@@ -168,29 +170,24 @@ def tile_attend_keyframes_kernel(tc, query, keys, fr, fv, size, vals, vsc, offs,
         got2 = gather_values(2, "got2")
         p_exp = sb.tile([P, I], F32)
         row_sum = sb.tile([P, 1], F32)
-        nc.scalar.activation(p_exp[:], scores[:], ACT.Exp, bias=neg_max[:], scale=1.0, accum_out=row_sum[:])
+        nc.scalar.activation(p_exp[:].rearrange("q (j g r) -> q j g r", j=4, r=8),
+                             scores[:].rearrange("q (g j r) -> q j g r", j=4, r=8), ACT.Exp, bias=neg_max[:], scale=1.0, accum_out=row_sum[:])
         turned1 = weigh_and_turn(1, got1, "part1_1", "k_second")
         got3 = gather_values(3, "neg_max")
         inv_sum = sb.tile([P, 1], F32, tag="got1")
         nc.vector.reciprocal(inv_sum[:], row_sum[:])
-        p_size = sb.tile([P, I], F32)
-        nc.gpsimd.tensor_tensor(p_size[:], p_exp[:], size_row[:], ALU.mult)
         w = sb.tile([P, I], BF16)
-        nc.gpsimd.tensor_scalar(dealt4(w[:]), slots4(p_size[:]), inv_sum[:], 0.0, ALU.mult, ALU.add)
+        nc.vector.scalar_tensor_tensor(w[:], p_exp[:], inv_sum[:], size_bank[:], ALU.mult, ALU.mult)
         w_turned = ps.tile([P, PACK, Q], BF16, tag="bank1", name="w_turned")
         for j in range(PACK):
             nc.tensor.transpose(w_turned[:, j, :], w[:, j * P:(j + 1) * P], ident_bf[:])
         turned2 = weigh_and_turn(2, got2, "part1_2", "part2_2")
         turned3 = weigh_and_turn(3, got3, "part1_3", "part2_3")
-        by_scalar = sb.tile([P, 4, PACK * P], BF16, tag="val3", align_bytes=64)
-        vv_bf[0] = by_scalar[:, 3, :]
-        vv_bf[1] = by_scalar[:, 1, :]
-        vv_bf[3] = by_scalar[:, 2, :]
+        rounded = sb.tile([P, PACK + 1, PACK * P], BF16, tag="val3", align_bytes=64)
         round_values(2, turned2, nc.vector.tensor_copy)
         round_values(0, turned0, nc.scalar.copy)
-        quantise_values(2)
         quantise_values(0)
-        wt_bf = by_scalar[:, 0, :]
+        wt_bf = rounded[:, PACK, :]
         nc.scalar.copy(out=wt_bf.rearrange("p (q j) -> p q j", j=PACK), in_=w_turned[:].rearrange("p j q -> p q j"))
         wt_codes = sb.tile([P, Q], U32, align_bytes=64)
         wt_scales = sb.tile([P, Q], U8, align_bytes=64)
@@ -199,6 +196,7 @@ def tile_attend_keyframes_kernel(tc, query, keys, fr, fv, size, vals, vsc, offs,
         round_values(1, turned1, nc.scalar.copy)
         quantise_values(1)
         round_values(3, turned3, nc.scalar.copy)
+        quantise_values(2)
         quantise_values(3)
 
         def product(acc, e0, n):

from contextlib import ExitStack

import concourse.mybir as mybir
from concourse.masks import make_identity

D, T, I, Q, E = 512, 1024, 512, 128, 512
FLOPS = 2 * Q * I * D + 2 * Q * I * E

F32 = mybir.dt.float32
BF16 = mybir.dt.bfloat16
U32 = mybir.dt.uint32
U16 = mybir.dt.uint16
U8 = mybir.dt.uint8
FP8X4 = mybir.dt.float8_e4m3fn_x4
ALU = mybir.AluOpType
ACT = mybir.ActivationFunctionType

P = 128
PACK = 4
TURN_BANKS = ("bank5", "bank6", "bank7", "bank0")


def tile_attend_keyframes_kernel(tc, query, keys, fr, fv, size, vals, vsc, offs, offs2, out):
    nc = tc.nc
    with ExitStack() as ctx:
        sb = ctx.enter_context(tc.tile_pool(name="sb", bufs=1))
        ps = ctx.enter_context(tc.psum_pool(name="ps", bufs=1))

        key_planes = keys.rearrange("(p j) t -> j p t", j=PACK)
        key = [sb.tile([P, T], F32, tag=f"key{j}", name=f"key{j}") for j in range(PACK)]
        val = [sb.tile([P, T], F32, tag=f"val{c}", name=f"val{c}", align_bytes=64) for c in range(PACK)]
        list1 = sb.tile([P, I // 16], U16)
        list2 = sb.tile([P, I // 16], U16)
        fr_col = sb.tile([P, PACK], F32)
        fv_col = sb.tile([P, PACK], F32)
        vsc_col = sb.tile([P, PACK], F32)
        size_col = sb.tile([P, PACK], F32)
        q_raw = sb.tile([P, PACK, Q], F32)

        nc.sync.dma_start(out=fr_col[:], in_=fr.rearrange("o (p c) -> p (o c)", c=PACK))
        nc.sync.dma_start(out=key[0][:], in_=key_planes[0])
        nc.sync.dma_start(list2[:], offs2)
        nc.sync.dma_start(list1[:], offs)
        nc.sync.dma_start(out=key[1][:], in_=key_planes[1])
        nc.sync.dma_start(out=fv_col[:], in_=fv.rearrange("(p c) o -> p (c o)", c=PACK))
        nc.sync.dma_start(out=vsc_col[:], in_=vsc.rearrange("(p c) o -> p (c o)", c=PACK))
        nc.sync.dma_start(out=key[2][:], in_=key_planes[2])
        nc.sync.dma_start(out=key[3][:], in_=key_planes[3])
        nc.sync.dma_start(out=size_col[:], in_=size.rearrange("o (p c) -> p (o c)", c=PACK))
        nc.sync.dma_start(out=val[0][:], in_=vals[0:P, :])
        nc.sync.dma_start(out=q_raw[:], in_=query.rearrange("(p j) q -> p j q", j=PACK))
        for c in range(1, PACK):
            nc.sync.dma_start(out=val[c][:], in_=vals[c * P:(c + 1) * P, :])

        ident = sb.tile([P, P], F32)
        make_identity(nc, ident[:])
        ident_bf = sb.tile([P, P], BF16)
        nc.scalar.activation(ident_bf[:], ident[:], ACT.Copy)

        def spread(col, tag, name):
            bank = ps.tile([P, PACK, P], F32, tag=tag, name=name)
            for c in range(PACK):
                nc.tensor.transpose(bank[:, c, :], col[:, c:c + 1].to_broadcast([P, P]), ident[:])
            return bank

        def in_slot_order(bank):
            return bank[:].rearrange("m c p -> m p c")

        def slots4(ap):
            return ap.rearrange("m (g j r c) -> m g j r c", j=4, r=2, c=4)

        def dealt4(ap):
            return ap.rearrange("m (j g r c) -> m g j r c", j=4, r=2, c=4)

        def bank4(bank):
            return bank[:].rearrange("m c (g j r) -> m g j r c", j=4, r=2)

        fr_bank = spread(fr_col, "bank0", "fr_bank")
        fr_row = sb.tile([P, I], F32)
        nc.vector.tensor_copy(out=fr_row[:].rearrange("m (p c) -> m p c", c=PACK), in_=in_slot_order(fr_bank))
        omf_col = sb.tile([P, PACK], F32)
        nc.scalar.activation(omf_col[:], fr_col[:], ACT.Copy, bias=1.0, scale=-1.0)
        omf_bank = spread(omf_col, "bank1", "omf_bank")

        k_first = sb.tile([P, PACK, I], F32, tag="key0")
        k_second = sb.tile([P, PACK, I], F32, tag="k_second")
        k_got = [sb.tile([P, I], F32, name=f"k_got{j}") for j in range(PACK)]
        omv_col = sb.tile([P, PACK], F32)
        a_col = sb.tile([P, PACK], F32)
        b_col = sb.tile([P, PACK], F32)
        for j in range(PACK):
            nc.scalar.activation(k_got[j][:], key[j][:].indirect(list1[:]), ACT.Copy)
            nc.vector.tensor_tensor(k_second[:, j, :], key[j][:].indirect(list2[:]), fr_row[:], ALU.mult)
            nc.vector.tensor_tensor(
                k_first[:, j, :].rearrange("m (p c) -> m p c", c=PACK),
                k_got[j][:].rearrange("m (p c) -> m p c", c=PACK), in_slot_order(omf_bank), ALU.mult)
            if j == 1:
                nc.gpsimd.tensor_scalar(omv_col[:], fv_col[:], -1.0, 1.0, ALU.mult, ALU.add)
                nc.gpsimd.tensor_tensor(b_col[:], fv_col[:], vsc_col[:], ALU.mult)
                nc.gpsimd.tensor_tensor(a_col[:], omv_col[:], vsc_col[:], ALU.mult)
        a_bank = spread(a_col, "bank2", "a_bank")
        b_bank = spread(b_col, "bank3", "b_bank")
        size_bank = ps.tile([P, I], F32, tag="bank4", name="size_bank")
        size_places = size_bank[:].rearrange("m (j g r c) -> m c g j r", j=4, r=2, c=4)
        for c in range(PACK):
            nc.tensor.transpose(size_places[:, c], size_col[:, c:c + 1].to_broadcast([P, P]), ident[:])

        q_bf = sb.tile([P, Q, PACK], BF16, align_bytes=64)
        nc.vector.tensor_copy(
            out=q_bf[:].rearrange("p (c i) j -> p c j i", i=4), in_=q_raw[:].rearrange("p j (c i) -> p c j i", i=4))
        km_bf = sb.tile([P, I, PACK], BF16, tag="km_bf", align_bytes=64)
        nc.vector.tensor_tensor(
            km_bf[:].rearrange("p (c i) j -> p c j i", i=4),
            k_first[:].rearrange("p j (c i) -> p c j i", i=4),
            k_second[:].rearrange("p j (c i) -> p c j i", i=4), ALU.add)
        q_codes = sb.tile([P, Q], U32, align_bytes=64)
        q_scales = sb.tile([P, Q], U8, align_bytes=64)
        nc.vector.quantize_mx(out=q_codes[:].bitcast(FP8X4), scales=q_scales[:],
                              in_=q_bf[:].rearrange("p q j -> p (q j)"))
        km_codes = sb.tile([P, I], U32, align_bytes=64)
        km_scales = sb.tile([P, I], U8, align_bytes=64)
        nc.vector.quantize_mx(out=km_codes[:].bitcast(FP8X4), scales=km_scales[:],
                              in_=km_bf[:].rearrange("p i j -> p (i j)"))
        scores = ps.tile([P, I], F32, tag="bank0", name="scores")
        nc.tensor.matmul_mx(out=scores[:], lhsT=q_codes[:].bitcast(FP8X4), lhsT_scale=q_scales[:],
                            rhs=km_codes[:].bitcast(FP8X4), rhs_scale=km_scales[:], start=True, stop=True)

        vv_codes = sb.tile([P, E], U32, align_bytes=64)
        vv_scales = sb.tile([P, E], U8, align_bytes=64)

        def gather_values(c, tag):
            got = sb.tile([P, 2, I], F32, tag=tag, name=f"v_got{c}")
            nc.scalar.activation(got[:, 0, :], val[c][:].indirect(list1[:]), ACT.Copy)
            nc.scalar.activation(got[:, 1, :], val[c][:].indirect(list2[:]), ACT.Copy)
            return got

        def weigh_and_turn(c, got, tag1, tag2):
            part1 = sb.tile([P, I], F32, tag=tag1, name=f"v_part1_{c}", align_bytes=64)
            part2 = sb.tile([P, I], F32, tag=tag2, name=f"v_part2_{c}")
            nc.vector.tensor_tensor(dealt4(part1[:]), slots4(got[:, 0, :]), bank4(a_bank), ALU.mult)
            step = PACK // 2 if c == PACK - 1 else PACK
            for j0 in range(0, PACK, step):
                places = slice(j0, j0 + step)
                nc.vector.tensor_tensor(dealt4(part2[:])[:, :, places], slots4(got[:, 1, :])[:, :, places],
                                        bank4(b_bank)[:, :, places], ALU.mult)
            turned = ps.tile([P, PACK, P], F32, tag=TURN_BANKS[c], name=f"turned{c}")
            for j in range(PACK):
                nc.tensor.matmul(turned[:, j, :], lhsT=part1[:, j * P:(j + 1) * P], rhs=ident[:],
                                 start=(j == 0), stop=False, is_transpose=True)
            for j in range(PACK):
                nc.tensor.matmul(turned[:, j, :], lhsT=part2[:, j * P:(j + 1) * P], rhs=ident[:],
                                 start=False, stop=(j == PACK - 1), is_transpose=True)
            return turned

        def round_values(c, turned, copy):
            vv_bf = rounded[:, c, :].rearrange("p (e j) -> p e j", j=PACK)
            copy(out=vv_bf, in_=turned[:].rearrange("p j e -> p e j"))

        def quantise_values(c):
            nc.vector.quantize_mx(out=vv_codes[:, c * P:(c + 1) * P].bitcast(FP8X4),
                                  scales=vv_scales[:, c * P:(c + 1) * P],
                                  in_=rounded[:, c, :])

        got0 = gather_values(0, "got0")
        got1 = gather_values(1, "got1")
        turned0 = weigh_and_turn(0, got0, "km_bf", "key0")

        neg_max = sb.tile([P, 1], F32, tag="neg_max")
        nc.vector.tensor_reduce(neg_max[:], scores[:], mybir.AxisListType.X, ALU.max, negate=True)
        got2 = gather_values(2, "got2")
        p_exp = sb.tile([P, I], F32)
        row_sum = sb.tile([P, 1], F32)
        nc.scalar.activation(p_exp[:].rearrange("q (j g r) -> q j g r", j=4, r=8),
                             scores[:].rearrange("q (g j r) -> q j g r", j=4, r=8), ACT.Exp, bias=neg_max[:], scale=1.0, accum_out=row_sum[:])
        turned1 = weigh_and_turn(1, got1, "part1_1", "k_second")
        got3 = gather_values(3, "neg_max")
        inv_sum = sb.tile([P, 1], F32, tag="got1")
        nc.vector.reciprocal(inv_sum[:], row_sum[:])
        w = sb.tile([P, I], BF16)
        nc.vector.scalar_tensor_tensor(w[:], p_exp[:], inv_sum[:], size_bank[:], ALU.mult, ALU.mult)
        w_turned = ps.tile([P, PACK, Q], BF16, tag="bank1", name="w_turned")
        for j in range(PACK):
            nc.tensor.transpose(w_turned[:, j, :], w[:, j * P:(j + 1) * P], ident_bf[:])
        turned2 = weigh_and_turn(2, got2, "part1_2", "part2_2")
        turned3 = weigh_and_turn(3, got3, "part1_3", "part2_3")
        rounded = sb.tile([P, PACK + 1, PACK * P], BF16, tag="val3", align_bytes=64)
        round_values(2, turned2, nc.vector.tensor_copy)
        round_values(0, turned0, nc.scalar.copy)
        quantise_values(0)
        wt_bf = rounded[:, PACK, :]
        nc.scalar.copy(out=wt_bf.rearrange("p (q j) -> p q j", j=PACK), in_=w_turned[:].rearrange("p j q -> p q j"))
        wt_codes = sb.tile([P, Q], U32, align_bytes=64)
        wt_scales = sb.tile([P, Q], U8, align_bytes=64)
        nc.vector.quantize_mx(out=wt_codes[:].bitcast(FP8X4), scales=wt_scales[:],
                              in_=wt_bf)
        round_values(1, turned1, nc.scalar.copy)
        quantise_values(1)
        round_values(3, turned3, nc.scalar.copy)
        quantise_values(2)
        quantise_values(3)

        def product(acc, e0, n):
            nc.tensor.matmul_mx(out=acc, lhsT=wt_codes[:].bitcast(FP8X4), lhsT_scale=wt_scales[:],
                                rhs=vv_codes[:, e0:e0 + n].bitcast(FP8X4), rhs_scale=vv_scales[:, e0:e0 + n],
                                start=True, stop=True)

        last = E - P
        acc0 = ps.tile([P, last], F32, tag="bank4", name="acc0")
        product(acc0[:, 0:2 * P], 0, 2 * P)
        product(acc0[:, 2 * P:last], 2 * P, P)
        res0 = sb.tile([P, last], F32)
        nc.scalar.copy(out=res0[:], in_=acc0[:])
        nc.scalar.dma_start(out=out[:, 0:last], in_=res0[:])
        acc1 = ps.tile([P, P], F32, tag="bank5", name="acc1")
        product(acc1[:], last, P)
        res1 = sb.tile([P, P], F32)
        nc.vector.tensor_copy(out=res1[:], in_=acc1[:])
        nc.sync.dma_start(out=out[:, last:E], in_=res1[:])
